import numpy as np
import ml_dtypes


def mxq(x, axis, fmt="e4m3"):
    dtype, down = {"e4m3": (ml_dtypes.float8_e4m3fn, 7), "e5m2": (ml_dtypes.float8_e5m2, 14)}[fmt]
    v = np.moveaxis(np.asarray(x, np.float32).astype(ml_dtypes.bfloat16).astype(np.float64), axis, -1)
    blocks = v.reshape(v.shape[:-1] + (-1, 32))
    amax = np.abs(blocks).max(-1, keepdims=True)
    byte = np.maximum(np.where(amax > 0, np.frexp(amax)[1] - 1 + 127, 0) - down, 1)
    scale = np.exp2(byte - 127.0)
    codes = (blocks / scale).astype(np.float32).astype(dtype).astype(np.float64)
    return np.moveaxis((codes * scale).reshape(v.shape), -1, axis)


WIDE = False


def mx_kscale(k):
    if not WIDE:
        return np.ones(k)
    levels = np.array([10, -10, 5, -5, 0])
    if k % 512:
        return np.exp2(np.random.permutation(np.resize(levels, k // 32))).repeat(32)
    a = np.empty((k // 512, 16))
    for p in range(k // 512):
        a[p, :8] = np.random.permutation(np.resize(levels, 8))
        for g in range(8):
            far = levels[np.abs(levels - a[p, g]) >= 10]
            a[p, g + 8] = far[np.random.randint(len(far))]
    return np.exp2(a.ravel()).repeat(32)


def f64(x):
    return np.asarray(x).astype(np.float64)


def striped(idx):
    return np.tile(idx.reshape(-1, 16).T, (8, 1)).astype(np.uint16)


def unstriped(offs):
    return offs[:16].T.reshape(-1).astype(np.int64)


E2M1 = np.array([0.0, 0.5, 1.0, 1.5, 2.0, 3.0, 4.0, 6.0, -0.0, -0.5, -1.0, -1.5, -2.0, -3.0, -4.0, -6.0])


def pack_weight(w, fmt):
    k, n = w.shape
    w = f64(np.asarray(w, np.float32).astype(ml_dtypes.bfloat16)).reshape(k // 32, 32, n)
    amax = np.abs(w).max(1)
    if fmt == "e4m3":
        byte = np.frexp(amax)[1] - 1 + 127 - 7
    else:
        mant, ex = np.frexp(amax / 6.0)
        byte = np.where(mant > 0.5, ex, ex - 1) + 127
    byte = np.clip(np.where(amax > 0, byte, 1), 1, 254)
    scaled = (w * np.exp2(127.0 - byte)[:, None, :]).reshape(k, n).astype(np.float32)
    by_word = np.ascontiguousarray(scaled.reshape(k // 512, 128, 4, n).transpose(0, 1, 3, 2))
    if fmt == "e4m3":
        words = by_word.astype(ml_dtypes.float8_e4m3fn).view(np.uint8)
    else:
        c = by_word.astype(ml_dtypes.float4_e2m1fn).view(np.uint8) & 0xF
        words = (c[..., 0::2] | (c[..., 1::2] << 4)).reshape(k // 512, 128, 2 * n)
    return np.ascontiguousarray(words), np.ascontiguousarray(byte.astype(np.uint8).reshape(k // 512, 16, n))


def unpack_weight(words, scales, fmt):
    g, _, n = scales.shape
    words = np.ascontiguousarray(words).reshape(g, 128, n, -1)
    if fmt == "e4m3":
        vals = words.view(ml_dtypes.float8_e4m3fn).astype(np.float64)
    else:
        nib = np.empty((g, 128, n, 4), np.uint8)
        nib[..., 0::2] = words & 0xF
        nib[..., 1::2] = words >> 4
        vals = E2M1[nib]
    vals = vals * np.repeat(np.exp2(scales.astype(np.float64) - 127.0), 8, axis=1)[..., None]
    return vals.transpose(0, 1, 3, 2).reshape(g * 512, n)


def relu(v):
    return np.maximum(v, 0.0)


K, T, E, C, H, N = 1024, 2048, 8, 256, 512, 128


def by_expert(wq, xq):
    return np.concatenate([wq[e].T @ xq[:, e * C:(e + 1) * C] for e in range(E)], axis=1)


def setup_inputs():
    n = np.random.standard_normal
    s = mx_kscale(K)[:, None]
    u = mx_kscale(H)
    w1 = [pack_weight(m, "e2m1") for m in n((E, K, H)) / np.sqrt(K) / s[None] * u[None, None, :]]
    w2 = [pack_weight(m, "e2m1") for m in n((E, H, N)) / np.sqrt(H) / u[None, :, None]]
    return {
        "xT": (n((K, T)) * s).astype(np.float32),
        "w1_words": np.stack([m[0] for m in w1]),
        "w1_scales": np.stack([m[1] for m in w1]),
        "w2_words": np.stack([m[0] for m in w2]),
        "w2_scales": np.stack([m[1] for m in w2]),
        "gate": np.tile(np.random.uniform(0.2, 1.0, E * C), (N, 1)).astype(np.float32),
        "offs": striped(np.random.permutation(T)[:E * C]),
        "dst": striped(np.random.permutation(T)[:E * C]),
    }


def reference(xT, w1_words, w1_scales, w2_words, w2_scales, gate, offs, dst):
    idx = unstriped(offs)
    w1 = np.stack([unpack_weight(w1_words[e], w1_scales[e], "e2m1") for e in range(E)])
    w2 = np.stack([unpack_weight(w2_words[e], w2_scales[e], "e2m1") for e in range(E)])
    xq = mxq(f64(xT)[:, idx], 0, "e4m3")
    h = relu(by_expert(w1, xq))
    y = by_expert(w2, mxq(h, 0, "e4m3"))
    out = np.zeros((N, T))
    out[:, unstriped(dst)] = f64(gate) * y
    return out

@@ -1,0 +1,171 @@
+from contextlib import ExitStack
+
+import concourse.mybir as mybir
+from concourse.masks import make_identity
+
+K, T, E, C, H, N = 1024, 2048, 8, 256, 512, 128
+FLOPS = 2 * E * C * (K * H + H * N)
+
+F32 = mybir.dt.float32
+BF16 = mybir.dt.bfloat16
+I32 = mybir.dt.int32
+U32 = mybir.dt.uint32
+U16 = mybir.dt.uint16
+U8 = mybir.dt.uint8
+FP8X4 = mybir.dt.float8_e4m3fn_x4
+FP4X4 = mybir.dt.float4_e2m1fn_x4
+RELU = mybir.ActivationFunctionType.Relu
+MULT = mybir.AluOpType.mult
+
+P = 128
+PASSES = K // 512
+GATHERS = {0: (0, 256), 1: (256, 256), 2: (512, 512), 4: (1024, 512), 6: (1536, 512)}
+CHUNKS = {0: ((0, 512, 320), (512, 512, 320), (1024, 512, 320), (1536, 256, 160), (1792, 256, 160)),
+          1: ((0, 512, 0), (512, 512, 0), (1024, 512, 0), (1536, 256, 0), (1792, 256, 128))}
+
+
+def tile_moe_two_mlp_relu_kernel(tc, xT, w1_words, w1_scales, w2_words, w2_scales, gate, offs, dst, out):
+    nc = tc.nc
+    with ExitStack() as ctx:
+        lists = ctx.enter_context(tc.tile_pool(name="lists", bufs=1))
+        keep = ctx.enter_context(tc.tile_pool(name="keep", bufs=1))
+        psum_a = ctx.enter_context(tc.psum_pool(name="psum_a", bufs=4))
+        psum_t = ctx.enter_context(tc.psum_pool(name="psum_t", bufs=2))
+        psum_y = ctx.enter_context(tc.psum_pool(name="psum_y", bufs=2))
+
+        offs_t = lists.tile([P, T // 16], U16, name="offs_t")
+        dst_t = lists.tile([P, T // 16], U16, name="dst_t")
+
+        words = [keep.tile([P, T], U32, name=f"words{s}", align_bytes=64) for s in range(PASSES)]
+        bytes_ = [keep.tile([P, T], U8, name=f"scales{s}", align_bytes=64) for s in range(PASSES)]
+        slot_words = [keep.tile([P, T], U32, name=f"slot_words{s}", align_bytes=64) for s in range(PASSES)]
+        slot_bytes = [keep.tile([P, T], U8, name=f"slot_scales{s}", align_bytes=64) for s in range(PASSES)]
+        w1w = keep.tile([P, E * PASSES, 2 * H], U8, name="w1w", align_bytes=64)
+        w1s = keep.tile([P, E * PASSES, H], U8, name="w1s", align_bytes=64)
+        w2w = keep.tile([P, E, 2 * N], U8, name="w2w", align_bytes=64)
+        w2s = keep.tile([P, E, N], U8, name="w2s", align_bytes=64)
+        gate_t = keep.tile([P, T], F32, name="gate_t")
+        out_t = keep.tile([P, T], F32, name="out_t")
+        ident = keep.tile([P, P], F32, name="ident")
+
+        nc.gpsimd.memset(bytes_[0][:], 0)
+        nc.gpsimd.memset(w1s[:].rearrange("p a b -> p (a b)").bitcast(I32), 0)
+        nc.gpsimd.memset(w2s[:].rearrange("p a b -> p (a b)").bitcast(I32), 0)
+        nc.gpsimd.memset(bytes_[1][:], 0)
+        make_identity(nc, ident[:])
+
+        raw, grouped = {}, {}
+        for s in range(PASSES):
+            for c, (c0, w, v) in enumerate(CHUNKS[s]):
+                raw[s, c] = keep.tile([P, 4, w], F32, name=f"raw{s}_{c}")
+                grouped[s, c] = keep.tile([P, w, 4], BF16, name=f"grouped{s}_{c}", align_bytes=64)
+                nc.sync.dma_start(out=raw[s, c][:], in_=xT[512 * s : 512 * s + 512, c0 : c0 + w].rearrange("(p j) w -> p j w", j=4))
+                if s == 0 and c == 1:
+                    nc.sync.dma_start(offs_t[:], offs)
+
+        def load_w1(e):
+            nc.sync.dma_start(
+                out=w1w[:, 2 * e : 2 * e + 4, :].bitcast(I32),
+                in_=w1_words[e : e + 2].rearrange("e s p b -> p (e s) b").bitcast(I32),
+            )
+
+        w1s_rows = w1_scales.rearrange("e s (q r) i -> r q (e s) i", r=4)
+        w2s_rows = w2_scales.rearrange("e s (q r) i -> r q (e s) i", r=4)
+        for r in range(4):
+            nc.sync.dma_start(out=w1s[r:128:32, :, :].bitcast(I32), in_=w1s_rows[r].bitcast(I32))
+        for r in range(4):
+            nc.sync.dma_start(out=w2s[r:128:32, :, :].bitcast(I32), in_=w2s_rows[r].bitcast(I32))
+        load_w1(0)
+        load_w1(2)
+        nc.sync.dma_start(out=w2w[:].bitcast(I32), in_=w2_words.rearrange("e s p b -> p (e s) b").bitcast(I32))
+        nc.sync.dma_start(dst_t[:], dst)
+        load_w1(4)
+        nc.sync.dma_start(out=gate_t[:, : T // 2], in_=gate[:, : T // 2])
+        load_w1(6)
+        nc.sync.dma_start(out=gate_t[:, T // 2 :], in_=gate[:, T // 2 :])
+
+        def cast(engine, s, c, lo, hi):
+            if hi > lo:
+                engine(
+                    grouped[s, c][:, lo:hi, :].rearrange("p (b i) j -> p b j i", i=4),
+                    raw[s, c][:, :, lo:hi].rearrange("p j (b i) -> p b j i", i=4),
+                )
+
+        def quantise(s, c):
+            c0, w, v = CHUNKS[s][c]
+            nc.vector.quantize_mx(
+                out=words[s][:, c0 : c0 + w].bitcast(FP8X4),
+                scales=bytes_[s][:, c0 : c0 + w],
+                in_=grouped[s, c][:].rearrange("p w j -> p (w j)"),
+            )
+
+        def gather(dest, table, lo, n):
+            nc.vector.tensor_copy(dest[:, lo : lo + n], table[:].indirect(offs_t[:, lo // 16 : (lo + n) // 16]))
+
+        for c, (c0, w, v) in enumerate(CHUNKS[0]):
+            cast(nc.vector.tensor_copy, 0, c, 0, v)
+            cast(nc.scalar.copy, 0, c, v, w)
+            quantise(0, c)
+
+        for c, (c0, w, v) in enumerate(CHUNKS[1]):
+            cast(nc.scalar.copy, 1, c, v, w)
+        gather(slot_words[0], words[0], 0, 1024)
+        gather(slot_words[0], words[0], 1024, 1024)
+        quantise(1, 0)
+        gather(slot_bytes[0], bytes_[0], 0, 1024)
+        quantise(1, 1)
+        gather(slot_bytes[0], bytes_[0], 1024, 1024)
+        quantise(1, 2)
+        quantise(1, 3)
+        cast(nc.vector.tensor_copy, 1, 4, 0, CHUNKS[1][4][2])
+        quantise(1, 4)
+
+        ys = []
+        for e in range(E):
+            if e in GATHERS:
+                gather(slot_words[1], words[1], *GATHERS[e])
+                gather(slot_bytes[1], bytes_[1], *GATHERS[e])
+            hg = keep.tile([P, C, 4], BF16, name=f"hg{e}", align_bytes=64)
+            hg_words = hg[:].rearrange("p c t -> p (c t)").bitcast(F32).rearrange("p (c u) -> p c u", u=2)
+            tp = psum_t.tile([P, 2, C], F32, name="tp")
+            hs = []
+            for b in range(2):
+                cols = slice(C * e + P * b, C * e + P * b + P)
+                acc = psum_a.tile([P, H], F32, name="acc")
+                for s in range(PASSES):
+                    nc.tensor.matmul_mx(
+                        out=acc[:],
+                        lhsT=slot_words[s][:, cols].bitcast(FP8X4),
+                        lhsT_scale=slot_bytes[s][:, cols],
+                        rhs=w1w[:, 2 * e + s, :].bitcast(FP4X4),
+                        rhs_scale=w1s[:, 2 * e + s, :],
+                        start=(s == 0),
+                        stop=(s == PASSES - 1),
+                    )
+                hs.append(keep.tile([P, 2, P, 2], BF16, name=f"hs{e}_{b}"))
+                nc.scalar.activation(hs[b][:], acc[:].rearrange("c (p u e) -> c u p e", u=2, e=2), RELU)
+            for b in range(2):
+                turned = hs[b][:].rearrange("c u p e -> c u (p e)").bitcast(F32)
+                for u in range(2):
+                    nc.tensor.transpose(tp[:, u, P * b : P * b + P], turned[:, u, :], ident[:])
+            nc.scalar.copy(hg_words, tp[:].rearrange("p u r -> p r u"))
+            hq = keep.tile([P, C], U32, name=f"hq{e}", align_bytes=64)
+            hqs = keep.tile([P, C], U8, name=f"hqs{e}", align_bytes=64)
+            nc.vector.quantize_mx(out=hq[:].bitcast(FP8X4), scales=hqs[:], in_=hg[:].rearrange("p c t -> p (c t)"))
+            y = psum_y.tile([P, C], F32, name="y")
+            nc.tensor.matmul_mx(
+                out=y[:],
+                lhsT=w2w[:, e, :].bitcast(FP4X4),
+                lhsT_scale=w2s[:, e, :],
+                rhs=hq[:].bitcast(FP8X4),
+                rhs_scale=hqs[:],
+                start=True,
+                stop=True,
+            )
+            ys.append(keep.tile([P, C], F32, name=f"ys{e}"))
+            nc.scalar.copy(ys[e][:], y[:])
+
+        for e in range(E):
+            cols = slice(C * e, C * e + C)
+            nc.vector.tensor_tensor(out_t[:].indirect(dst_t[:, C * e // 16 : C * (e + 1) // 16]), ys[e][:], gate_t[:, cols], MULT)
+        nc.sync.dma_start(out=out, in_=out_t[:])

@@ -19,7 +19,7 @@ MULT = mybir.AluOpType.mult
 
 P = 128
 PASSES = K // 512
-GATHERS = {0: (0, 256), 1: (256, 256), 2: (512, 512), 4: (1024, 512), 6: (1536, 512)}
+UNITS = ((0, 256), (256, 256), (512, 512), (1024, 512), (1536, 512))
 CHUNKS = {0: ((0, 512, 320), (512, 512, 320), (1024, 512, 320), (1536, 256, 160), (1792, 256, 160)),
           1: ((0, 512, 0), (512, 512, 0), (1024, 512, 0), (1536, 256, 0), (1792, 256, 128))}
 
@@ -55,13 +55,14 @@ def tile_moe_two_mlp_relu_kernel(tc, xT, w1_words, w1_scales, w2_words, w2_scale
         make_identity(nc, ident[:])
 
         raw, grouped = {}, {}
-        for s in range(PASSES):
-            for c, (c0, w, v) in enumerate(CHUNKS[s]):
-                raw[s, c] = keep.tile([P, 4, w], F32, name=f"raw{s}_{c}")
-                grouped[s, c] = keep.tile([P, w, 4], BF16, name=f"grouped{s}_{c}", align_bytes=64)
-                nc.sync.dma_start(out=raw[s, c][:], in_=xT[512 * s : 512 * s + 512, c0 : c0 + w].rearrange("(p j) w -> p j w", j=4))
-                if s == 0 and c == 1:
-                    nc.sync.dma_start(offs_t[:], offs)
+        w1s_rows = w1_scales.rearrange("e s (q r) i -> r q (e s) i", r=4)
+        w2s_rows = w2_scales.rearrange("e s (q r) i -> r q (e s) i", r=4)
+
+        def load_x(s, c):
+            c0, w, v = CHUNKS[s][c]
+            raw[s, c] = keep.tile([P, 4, w], F32, name=f"raw{s}_{c}")
+            grouped[s, c] = keep.tile([P, w, 4], BF16, name=f"grouped{s}_{c}", align_bytes=64)
+            nc.sync.dma_start(out=raw[s, c][:], in_=xT[512 * s : 512 * s + 512, c0 : c0 + w].rearrange("(p j) w -> p j w", j=4))
 
         def load_w1(e):
             nc.sync.dma_start(
@@ -69,18 +70,24 @@ def tile_moe_two_mlp_relu_kernel(tc, xT, w1_words, w1_scales, w2_words, w2_scale
                 in_=w1_words[e : e + 2].rearrange("e s p b -> p (e s) b").bitcast(I32),
             )
 
-        w1s_rows = w1_scales.rearrange("e s (q r) i -> r q (e s) i", r=4)
-        w2s_rows = w2_scales.rearrange("e s (q r) i -> r q (e s) i", r=4)
+        for c in range(5):
+            load_x(0, c)
+            if c == 1:
+                nc.sync.dma_start(offs_t[:], offs)
+        for c in range(3):
+            load_x(1, c)
         for r in range(4):
             nc.sync.dma_start(out=w1s[r:128:32, :, :].bitcast(I32), in_=w1s_rows[r].bitcast(I32))
+        load_w1(0)
+        for c in range(3, 5):
+            load_x(1, c)
+        load_w1(2)
         for r in range(4):
             nc.sync.dma_start(out=w2s[r:128:32, :, :].bitcast(I32), in_=w2s_rows[r].bitcast(I32))
-        load_w1(0)
-        load_w1(2)
         nc.sync.dma_start(out=w2w[:].bitcast(I32), in_=w2_words.rearrange("e s p b -> p (e s) b").bitcast(I32))
         nc.sync.dma_start(dst_t[:], dst)
-        load_w1(4)
         nc.sync.dma_start(out=gate_t[:, : T // 2], in_=gate[:, : T // 2])
+        load_w1(4)
         load_w1(6)
         nc.sync.dma_start(out=gate_t[:, T // 2 :], in_=gate[:, T // 2 :])
 
@@ -102,35 +109,21 @@ def tile_moe_two_mlp_relu_kernel(tc, xT, w1_words, w1_scales, w2_words, w2_scale
         def gather(dest, table, lo, n):
             nc.vector.tensor_copy(dest[:, lo : lo + n], table[:].indirect(offs_t[:, lo // 16 : (lo + n) // 16]))
 
-        for c, (c0, w, v) in enumerate(CHUNKS[0]):
-            cast(nc.vector.tensor_copy, 0, c, 0, v)
-            cast(nc.scalar.copy, 0, c, v, w)
-            quantise(0, c)
-
-        for c, (c0, w, v) in enumerate(CHUNKS[1]):
-            cast(nc.scalar.copy, 1, c, v, w)
-        gather(slot_words[0], words[0], 0, 1024)
-        gather(slot_words[0], words[0], 1024, 1024)
-        quantise(1, 0)
-        gather(slot_bytes[0], bytes_[0], 0, 1024)
-        quantise(1, 1)
-        gather(slot_bytes[0], bytes_[0], 1024, 1024)
-        quantise(1, 2)
-        quantise(1, 3)
-        cast(nc.vector.tensor_copy, 1, 4, 0, CHUNKS[1][4][2])
-        quantise(1, 4)
+        for s in range(PASSES):
+            for c, (c0, w, v) in enumerate(CHUNKS[s]):
+                cast(nc.vector.tensor_copy, s, c, 0, v)
+                cast(nc.scalar.copy, s, c, v, w)
+                quantise(s, c)
 
         ys = []
-        for e in range(E):
-            if e in GATHERS:
-                gather(slot_words[1], words[1], *GATHERS[e])
-                gather(slot_bytes[1], bytes_[1], *GATHERS[e])
-            hg = keep.tile([P, C, 4], BF16, name=f"hg{e}", align_bytes=64)
-            hg_words = hg[:].rearrange("p c t -> p (c t)").bitcast(F32).rearrange("p (c u) -> p c u", u=2)
-            tp = psum_t.tile([P, 2, C], F32, name="tp")
+        for n, (lo, width) in enumerate(UNITS):
+            for s in range(PASSES):
+                gather(slot_words[s], words[s], lo, width)
+                gather(slot_bytes[s], bytes_[s], lo, width)
             hs = []
-            for b in range(2):
-                cols = slice(C * e + P * b, C * e + P * b + P)
+            for j in range(lo // P, (lo + width) // P):
+                e = P * j // C
+                cols = slice(P * j, P * j + P)
                 acc = psum_a.tile([P, H], F32, name="acc")
                 for s in range(PASSES):
                     nc.tensor.matmul_mx(
@@ -142,30 +135,36 @@ def tile_moe_two_mlp_relu_kernel(tc, xT, w1_words, w1_scales, w2_words, w2_scale
                         start=(s == 0),
                         stop=(s == PASSES - 1),
                     )
-                hs.append(keep.tile([P, 2, P, 2], BF16, name=f"hs{e}_{b}"))
-                nc.scalar.activation(hs[b][:], acc[:].rearrange("c (p u e) -> c u p e", u=2, e=2), RELU)
-            for b in range(2):
-                turned = hs[b][:].rearrange("c u p e -> c u (p e)").bitcast(F32)
-                for u in range(2):
-                    nc.tensor.transpose(tp[:, u, P * b : P * b + P], turned[:, u, :], ident[:])
-            nc.scalar.copy(hg_words, tp[:].rearrange("p u r -> p r u"))
-            hq = keep.tile([P, C], U32, name=f"hq{e}", align_bytes=64)
-            hqs = keep.tile([P, C], U8, name=f"hqs{e}", align_bytes=64)
+                hs.append(keep.tile([P, 2, P, 2], BF16, name=f"hs{j}"))
+                nc.scalar.activation(hs[-1][:], acc[:].rearrange("c (p u e) -> c u p e", u=2, e=2), RELU)
+            hg = keep.tile([P, width, 4], BF16, name=f"hg{n}", align_bytes=64)
+            hg_words = hg[:].rearrange("p c t -> p (c t)").bitcast(F32).rearrange("p (c u) -> p c u", u=2)
+            for half in range(width // 256):
+                tp = psum_t.tile([P, 2, 256], F32, name="tp")
+                for b in range(2):
+                    turned = hs[2 * half + b][:].rearrange("c u p e -> c u (p e)").bitcast(F32)
+                    for u in range(2):
+                        nc.tensor.transpose(tp[:, u, P * b : P * b + P], turned[:, u, :], ident[:])
+                nc.scalar.copy(hg_words[:, 256 * half : 256 * half + 256, :], tp[:].rearrange("p u r -> p r u"))
+            hq = keep.tile([P, width], U32, name=f"hq{n}", align_bytes=64)
+            hqs = keep.tile([P, width], U8, name=f"hqs{n}", align_bytes=64)
             nc.vector.quantize_mx(out=hq[:].bitcast(FP8X4), scales=hqs[:], in_=hg[:].rearrange("p c t -> p (c t)"))
-            y = psum_y.tile([P, C], F32, name="y")
-            nc.tensor.matmul_mx(
-                out=y[:],
-                lhsT=w2w[:, e, :].bitcast(FP4X4),
-                lhsT_scale=w2s[:, e, :],
-                rhs=hq[:].bitcast(FP8X4),
-                rhs_scale=hqs[:],
-                start=True,
-                stop=True,
-            )
-            ys.append(keep.tile([P, C], F32, name=f"ys{e}"))
-            nc.scalar.copy(ys[e][:], y[:])
+            y = psum_y.tile([P, 512], F32, name="y")
+            for b in range(width // C):
+                e = lo // C + b
+                cols = slice(C * b, C * b + C)
+                nc.tensor.matmul_mx(
+                    out=y[:, cols],
+                    lhsT=w2w[:, e, :].bitcast(FP4X4),
+                    lhsT_scale=w2s[:, e, :],
+                    rhs=hq[:, cols].bitcast(FP8X4),
+                    rhs_scale=hqs[:, cols],
+                    start=True,
+                    stop=True,
+                )
+            ys.append(keep.tile([P, width], F32, name=f"ys{n}"))
+            nc.scalar.copy(ys[n][:], y[:, :width])
 
-        for e in range(E):
-            cols = slice(C * e, C * e + C)
-            nc.vector.tensor_tensor(out_t[:].indirect(dst_t[:, C * e // 16 : C * (e + 1) // 16]), ys[e][:], gate_t[:, cols], MULT)
+        for n, (lo, width) in enumerate(UNITS):
+            nc.vector.tensor_tensor(out_t[:].indirect(dst_t[:, lo // 16 : (lo + width) // 16]), ys[n][:], gate_t[:, lo : lo + width], MULT)
         nc.sync.dma_start(out=out, in_=out_t[:])

@@ -19,9 +19,16 @@ MULT = mybir.AluOpType.mult
 
 P = 128
 PASSES = K // 512
-UNITS = ((0, 256), (256, 256), (512, 512), (1024, 512), (1536, 512))
-CHUNKS = {0: ((0, 512, 320), (512, 512, 320), (1024, 512, 320), (1536, 256, 160), (1792, 256, 160)),
-          1: ((0, 512, 0), (512, 512, 0), (1024, 512, 0), (1536, 256, 0), (1792, 256, 128))}
+CHUNKS = (
+    ((0, 512, 128), (512, 512, 128), (1024, 512, 128), (1536, 256, 96), (1792, 256, 96)),
+    ((0, 512, 0), (512, 512, 0), (1024, 512, 0), (1536, 256, 0), (1792, 256, 64)),
+)
+GROUPS = (((0, 1024), (1024, 1024)), ((0, 256), (256, 256), (512, 512), (1024, 512), (1536, 512)))
+UNITS = ((0, 256), (256, 256), (512, 256), (768, 256), (1024, 256), (1280, 256), (1536, 256), (1792, 256))
+SCATTERS = ((0, 512), (512, 512), (1024, 256), (1280, 256), (1536, 256), (1792, 256))
+TAGS = {"W0_1": "W1_0", "W1_3": "W1_2", "W1_4": "hg3"}
+YBANK = (1, 1, 2, 3, 1, 2, 2, 3)
+W1_AT = 5
 
 
 def tile_moe_two_mlp_relu_kernel(tc, xT, w1_words, w1_scales, w2_words, w2_scales, gate, offs, dst, out):
@@ -30,38 +37,36 @@ def tile_moe_two_mlp_relu_kernel(tc, xT, w1_words, w1_scales, w2_words, w2_scale
         lists = ctx.enter_context(tc.tile_pool(name="lists", bufs=1))
         keep = ctx.enter_context(tc.tile_pool(name="keep", bufs=1))
         psum_a = ctx.enter_context(tc.psum_pool(name="psum_a", bufs=4))
-        psum_t = ctx.enter_context(tc.psum_pool(name="psum_t", bufs=2))
-        psum_y = ctx.enter_context(tc.psum_pool(name="psum_y", bufs=2))
+        psum_b = ctx.enter_context(tc.psum_pool(name="psum_b", bufs=1))
 
         offs_t = lists.tile([P, T // 16], U16, name="offs_t")
         dst_t = lists.tile([P, T // 16], U16, name="dst_t")
 
-        words = [keep.tile([P, T], U32, name=f"words{s}", align_bytes=64) for s in range(PASSES)]
-        bytes_ = [keep.tile([P, T], U8, name=f"scales{s}", align_bytes=64) for s in range(PASSES)]
-        slot_words = [keep.tile([P, T], U32, name=f"slot_words{s}", align_bytes=64) for s in range(PASSES)]
-        slot_bytes = [keep.tile([P, T], U8, name=f"slot_scales{s}", align_bytes=64) for s in range(PASSES)]
-        w1w = keep.tile([P, E * PASSES, 2 * H], U8, name="w1w", align_bytes=64)
-        w1s = keep.tile([P, E * PASSES, H], U8, name="w1s", align_bytes=64)
-        w2w = keep.tile([P, E, 2 * N], U8, name="w2w", align_bytes=64)
-        w2s = keep.tile([P, E, N], U8, name="w2s", align_bytes=64)
-        gate_t = keep.tile([P, T], F32, name="gate_t")
-        out_t = keep.tile([P, T], F32, name="out_t")
-        ident = keep.tile([P, P], F32, name="ident")
+        def tile(name, shape, dtype):
+            return keep.tile(shape, dtype, name=name, tag=TAGS.get(name, name), align_bytes=64)
 
-        nc.gpsimd.memset(bytes_[0][:], 0)
+        words = [tile(f"words{s}", [P, T], U32) for s in range(PASSES)]
+        scales = [tile(f"scales{s}", [P, T], U8) for s in range(PASSES)]
+        w1w = tile("w1w", [P, E * PASSES, 2 * H], U8)
+        w1s = tile("w1s", [P, E * PASSES, H], U8)
+        w2w = tile("w2w", [P, E, 2 * N], U8)
+        w2s = tile("w2s", [P, E, N], U8)
+        gate_t = tile("gate_t", [P, T], F32)
+        out_t = tile("out_t", [P, T], F32)
+        ident = tile("ident", [P, P], F32)
+
+        nc.gpsimd.memset(scales[0][:], 0)
         nc.gpsimd.memset(w1s[:].rearrange("p a b -> p (a b)").bitcast(I32), 0)
         nc.gpsimd.memset(w2s[:].rearrange("p a b -> p (a b)").bitcast(I32), 0)
-        nc.gpsimd.memset(bytes_[1][:], 0)
+        nc.gpsimd.memset(scales[1][:], 0)
         make_identity(nc, ident[:])
 
         raw, grouped = {}, {}
-        w1s_rows = w1_scales.rearrange("e s (q r) i -> r q (e s) i", r=4)
-        w2s_rows = w2_scales.rearrange("e s (q r) i -> r q (e s) i", r=4)
 
         def load_x(s, c):
             c0, w, v = CHUNKS[s][c]
-            raw[s, c] = keep.tile([P, 4, w], F32, name=f"raw{s}_{c}")
-            grouped[s, c] = keep.tile([P, w, 4], BF16, name=f"grouped{s}_{c}", align_bytes=64)
+            raw[s, c] = tile(f"raw{s}_{c}", [P, 4, w], F32)
+            grouped[s, c] = tile(f"grouped{s}_{c}", [P, w, 4], BF16)
             nc.sync.dma_start(out=raw[s, c][:], in_=xT[512 * s : 512 * s + 512, c0 : c0 + w].rearrange("(p j) w -> p j w", j=4))
 
         def load_w1(e):
@@ -70,20 +75,23 @@ def tile_moe_two_mlp_relu_kernel(tc, xT, w1_words, w1_scales, w2_words, w2_scale
                 in_=w1_words[e : e + 2].rearrange("e s p b -> p (e s) b").bitcast(I32),
             )
 
-        for c in range(5):
+        def load_scales(plane, source):
+            rows = source.rearrange("e s (q r) i -> r q (e s) i", r=4)
+            for r in range(4):
+                nc.sync.dma_start(out=plane[r:P:32, :, :].bitcast(I32), in_=rows[r].bitcast(I32))
+
+        for c in range(len(CHUNKS[0])):
             load_x(0, c)
             if c == 1:
                 nc.sync.dma_start(offs_t[:], offs)
-        for c in range(3):
-            load_x(1, c)
-        for r in range(4):
-            nc.sync.dma_start(out=w1s[r:128:32, :, :].bitcast(I32), in_=w1s_rows[r].bitcast(I32))
-        load_w1(0)
-        for c in range(3, 5):
-            load_x(1, c)
+        for c in range(len(CHUNKS[1]) + 1):
+            if c == W1_AT:
+                load_scales(w1s, w1_scales)
+                load_w1(0)
+            if c < len(CHUNKS[1]):
+                load_x(1, c)
         load_w1(2)
-        for r in range(4):
-            nc.sync.dma_start(out=w2s[r:128:32, :, :].bitcast(I32), in_=w2s_rows[r].bitcast(I32))
+        load_scales(w2s, w2_scales)
         nc.sync.dma_start(out=w2w[:].bitcast(I32), in_=w2_words.rearrange("e s p b -> p (e s) b").bitcast(I32))
         nc.sync.dma_start(dst_t[:], dst)
         nc.sync.dma_start(out=gate_t[:, : T // 2], in_=gate[:, : T // 2])
@@ -98,73 +106,92 @@ def tile_moe_two_mlp_relu_kernel(tc, xT, w1_words, w1_scales, w2_words, w2_scale
                     raw[s, c][:, :, lo:hi].rearrange("p j (b i) -> p b j i", i=4),
                 )
 
-        def quantise(s, c):
-            c0, w, v = CHUNKS[s][c]
-            nc.vector.quantize_mx(
-                out=words[s][:, c0 : c0 + w].bitcast(FP8X4),
-                scales=bytes_[s][:, c0 : c0 + w],
-                in_=grouped[s, c][:].rearrange("p w j -> p (w j)"),
-            )
-
-        def gather(dest, table, lo, n):
-            nc.vector.tensor_copy(dest[:, lo : lo + n], table[:].indirect(offs_t[:, lo // 16 : (lo + n) // 16]))
-
         for s in range(PASSES):
             for c, (c0, w, v) in enumerate(CHUNKS[s]):
                 cast(nc.vector.tensor_copy, s, c, 0, v)
                 cast(nc.scalar.copy, s, c, v, w)
-                quantise(s, c)
+                nc.vector.quantize_mx(
+                    out=words[s][:, c0 : c0 + w].bitcast(FP8X4),
+                    scales=scales[s][:, c0 : c0 + w],
+                    in_=grouped[s, c][:].rearrange("p w j -> p (w j)"),
+                )
 
-        ys = []
-        for n, (lo, width) in enumerate(UNITS):
+        slot_words, slot_scales, hq, hqs, ys = {}, {}, {}, {}, {}
+
+        def gather(n):
             for s in range(PASSES):
-                gather(slot_words[s], words[s], lo, width)
-                gather(slot_bytes[s], bytes_[s], lo, width)
+                for g, (lo, w) in enumerate(GROUPS[s]):
+                    if lo == UNITS[n][0]:
+                        index = offs_t[:, lo // 16 : (lo + w) // 16]
+                        slot_words[s, g] = tile(f"W{s}_{g}", [P, w], U32)
+                        slot_scales[s, g] = tile(f"B{s}_{g}", [P, w], U8)
+                        nc.vector.tensor_copy(slot_words[s, g][:], words[s][:].indirect(index))
+                        nc.vector.tensor_copy(slot_scales[s, g][:], scales[s][:].indirect(index))
+
+        def of_slots(tiles, s, lo):
+            for g, (g0, w) in enumerate(GROUPS[s]):
+                if g0 <= lo < g0 + w:
+                    return tiles[s, g][:, lo - g0 : lo - g0 + P]
+
+        def first(n):
+            lo, w = UNITS[n]
             hs = []
-            for j in range(lo // P, (lo + width) // P):
-                e = P * j // C
-                cols = slice(P * j, P * j + P)
+            for b in range(w // P):
+                e = (lo + P * b) // C
                 acc = psum_a.tile([P, H], F32, name="acc")
                 for s in range(PASSES):
                     nc.tensor.matmul_mx(
                         out=acc[:],
-                        lhsT=slot_words[s][:, cols].bitcast(FP8X4),
-                        lhsT_scale=slot_bytes[s][:, cols],
+                        lhsT=of_slots(slot_words, s, lo + P * b).bitcast(FP8X4),
+                        lhsT_scale=of_slots(slot_scales, s, lo + P * b),
                         rhs=w1w[:, 2 * e + s, :].bitcast(FP4X4),
                         rhs_scale=w1s[:, 2 * e + s, :],
                         start=(s == 0),
                         stop=(s == PASSES - 1),
                     )
-                hs.append(keep.tile([P, 2, P, 2], BF16, name=f"hs{j}"))
-                nc.scalar.activation(hs[-1][:], acc[:].rearrange("c (p u e) -> c u p e", u=2, e=2), RELU)
-            hg = keep.tile([P, width, 4], BF16, name=f"hg{n}", align_bytes=64)
+                hs.append(tile(f"hs{n}_{b}", [P, 2, P, 2], BF16))
+                nc.scalar.activation(hs[b][:], acc[:].rearrange("c (p u e) -> c u p e", u=2, e=2), RELU)
+            hg = tile(f"hg{n}", [P, w, 4], BF16)
             hg_words = hg[:].rearrange("p c t -> p (c t)").bitcast(F32).rearrange("p (c u) -> p c u", u=2)
-            for half in range(width // 256):
-                tp = psum_t.tile([P, 2, 256], F32, name="tp")
+            for half in range(w // 256):
+                k = (lo + 256 * half) // 256
+                tp = psum_b.tile([P, 2, 256], F32, name=f"tp{k}", tag=f"bank{k % 4}")
                 for b in range(2):
                     turned = hs[2 * half + b][:].rearrange("c u p e -> c u (p e)").bitcast(F32)
                     for u in range(2):
                         nc.tensor.transpose(tp[:, u, P * b : P * b + P], turned[:, u, :], ident[:])
                 nc.scalar.copy(hg_words[:, 256 * half : 256 * half + 256, :], tp[:].rearrange("p u r -> p r u"))
-            hq = keep.tile([P, width], U32, name=f"hq{n}", align_bytes=64)
-            hqs = keep.tile([P, width], U8, name=f"hqs{n}", align_bytes=64)
-            nc.vector.quantize_mx(out=hq[:].bitcast(FP8X4), scales=hqs[:], in_=hg[:].rearrange("p c t -> p (c t)"))
-            y = psum_y.tile([P, 512], F32, name="y")
-            for b in range(width // C):
+            hq[n] = tile(f"hq{n}", [P, w], U32)
+            hqs[n] = tile(f"hqs{n}", [P, w], U8)
+            nc.vector.quantize_mx(out=hq[n][:].bitcast(FP8X4), scales=hqs[n][:], in_=hg[:].rearrange("p c t -> p (c t)"))
+
+        def second(n):
+            lo, w = UNITS[n]
+            y = psum_b.tile([P, 512], F32, name=f"y{n}", tag=f"bank{YBANK[n]}")
+            for b in range(w // C):
                 e = lo // C + b
                 cols = slice(C * b, C * b + C)
                 nc.tensor.matmul_mx(
                     out=y[:, cols],
                     lhsT=w2w[:, e, :].bitcast(FP4X4),
                     lhsT_scale=w2s[:, e, :],
-                    rhs=hq[:, cols].bitcast(FP8X4),
-                    rhs_scale=hqs[:, cols],
+                    rhs=hq[n][:, cols].bitcast(FP8X4),
+                    rhs_scale=hqs[n][:, cols],
                     start=True,
                     stop=True,
                 )
-            ys.append(keep.tile([P, width], F32, name=f"ys{n}"))
-            nc.scalar.copy(ys[n][:], y[:, :width])
+            for g, (g0, gw) in enumerate(SCATTERS):
+                if g0 <= lo < g0 + gw:
+                    if g not in ys:
+                        ys[g] = tile(f"ys{g}", [P, gw], F32)
+                    nc.scalar.copy(ys[g][:, lo - g0 : lo - g0 + w], y[:, :w])
 
-        for n, (lo, width) in enumerate(UNITS):
-            nc.vector.tensor_tensor(out_t[:].indirect(dst_t[:, lo // 16 : (lo + width) // 16]), ys[n][:], gate_t[:, lo : lo + width], MULT)
+        for n in range(len(UNITS)):
+            gather(n)
+            first(n)
+            if n >= 1:
+                second(n - 1)
+        second(len(UNITS) - 1)
+        for g, (lo, w) in enumerate(SCATTERS):
+            nc.vector.tensor_tensor(out_t[:].indirect(dst_t[:, lo // 16 : (lo + w) // 16]), ys[g][:], gate_t[:, lo : lo + w], MULT)
         nc.sync.dma_start(out=out, in_=out_t[:])

from contextlib import ExitStack

import concourse.mybir as mybir
from concourse.masks import make_identity

K, T, E, C, H, N = 1024, 2048, 8, 256, 512, 128
FLOPS = 2 * E * C * (K * H + H * N)

F32 = mybir.dt.float32
BF16 = mybir.dt.bfloat16
I32 = mybir.dt.int32
U32 = mybir.dt.uint32
U16 = mybir.dt.uint16
U8 = mybir.dt.uint8
FP8X4 = mybir.dt.float8_e4m3fn_x4
FP4X4 = mybir.dt.float4_e2m1fn_x4
RELU = mybir.ActivationFunctionType.Relu
MULT = mybir.AluOpType.mult

P = 128
PASSES = K // 512
CHUNKS = (
    ((0, 512, 128), (512, 512, 128), (1024, 512, 128), (1536, 256, 96), (1792, 256, 96)),
    ((0, 512, 0), (512, 512, 0), (1024, 512, 0), (1536, 256, 0), (1792, 256, 64)),
)
GROUPS = (((0, 1024), (1024, 1024)), ((0, 256), (256, 256), (512, 512), (1024, 512), (1536, 512)))
UNITS = ((0, 256), (256, 256), (512, 256), (768, 256), (1024, 256), (1280, 256), (1536, 256), (1792, 256))
SCATTERS = ((0, 512), (512, 512), (1024, 256), (1280, 256), (1536, 256), (1792, 256))
TAGS = {"W0_1": "W1_0", "W1_3": "W1_2", "W1_4": "hg3"}
YBANK = (1, 1, 2, 3, 1, 2, 2, 3)
W1_AT = 5


def tile_moe_two_mlp_relu_kernel(tc, xT, w1_words, w1_scales, w2_words, w2_scales, gate, offs, dst, out):
    nc = tc.nc
    with ExitStack() as ctx:
        lists = ctx.enter_context(tc.tile_pool(name="lists", bufs=1))
        keep = ctx.enter_context(tc.tile_pool(name="keep", bufs=1))
        psum_a = ctx.enter_context(tc.psum_pool(name="psum_a", bufs=4))
        psum_b = ctx.enter_context(tc.psum_pool(name="psum_b", bufs=1))

        offs_t = lists.tile([P, T // 16], U16, name="offs_t")
        dst_t = lists.tile([P, T // 16], U16, name="dst_t")

        def tile(name, shape, dtype):
            return keep.tile(shape, dtype, name=name, tag=TAGS.get(name, name), align_bytes=64)

        words = [tile(f"words{s}", [P, T], U32) for s in range(PASSES)]
        scales = [tile(f"scales{s}", [P, T], U8) for s in range(PASSES)]
        w1w = tile("w1w", [P, E * PASSES, 2 * H], U8)
        w1s = tile("w1s", [P, E * PASSES, H], U8)
        w2w = tile("w2w", [P, E, 2 * N], U8)
        w2s = tile("w2s", [P, E, N], U8)
        gate_t = tile("gate_t", [P, T], F32)
        out_t = tile("out_t", [P, T], F32)
        ident = tile("ident", [P, P], F32)

        nc.gpsimd.memset(scales[0][:], 0)
        nc.gpsimd.memset(w1s[:].rearrange("p a b -> p (a b)").bitcast(I32), 0)
        nc.gpsimd.memset(w2s[:].rearrange("p a b -> p (a b)").bitcast(I32), 0)
        nc.gpsimd.memset(scales[1][:], 0)
        make_identity(nc, ident[:])

        raw, grouped = {}, {}

        def load_x(s, c):
            c0, w, v = CHUNKS[s][c]
            raw[s, c] = tile(f"raw{s}_{c}", [P, 4, w], F32)
            grouped[s, c] = tile(f"grouped{s}_{c}", [P, w, 4], BF16)
            nc.sync.dma_start(out=raw[s, c][:], in_=xT[512 * s : 512 * s + 512, c0 : c0 + w].rearrange("(p j) w -> p j w", j=4))

        def load_w1(e):
            nc.sync.dma_start(
                out=w1w[:, 2 * e : 2 * e + 4, :].bitcast(I32),
                in_=w1_words[e : e + 2].rearrange("e s p b -> p (e s) b").bitcast(I32),
            )

        def load_scales(plane, source):
            rows = source.rearrange("e s (q r) i -> r q (e s) i", r=4)
            for r in range(4):
                nc.sync.dma_start(out=plane[r:P:32, :, :].bitcast(I32), in_=rows[r].bitcast(I32))

        for c in range(len(CHUNKS[0])):
            load_x(0, c)
            if c == 1:
                nc.sync.dma_start(offs_t[:], offs)
        for c in range(len(CHUNKS[1]) + 1):
            if c == W1_AT:
                load_scales(w1s, w1_scales)
                load_w1(0)
            if c < len(CHUNKS[1]):
                load_x(1, c)
        load_w1(2)
        load_scales(w2s, w2_scales)
        nc.sync.dma_start(out=w2w[:].bitcast(I32), in_=w2_words.rearrange("e s p b -> p (e s) b").bitcast(I32))
        nc.sync.dma_start(dst_t[:], dst)
        nc.sync.dma_start(out=gate_t[:, : T // 2], in_=gate[:, : T // 2])
        load_w1(4)
        load_w1(6)
        nc.sync.dma_start(out=gate_t[:, T // 2 :], in_=gate[:, T // 2 :])

        def cast(engine, s, c, lo, hi):
            if hi > lo:
                engine(
                    grouped[s, c][:, lo:hi, :].rearrange("p (b i) j -> p b j i", i=4),
                    raw[s, c][:, :, lo:hi].rearrange("p j (b i) -> p b j i", i=4),
                )

        for s in range(PASSES):
            for c, (c0, w, v) in enumerate(CHUNKS[s]):
                cast(nc.vector.tensor_copy, s, c, 0, v)
                cast(nc.scalar.copy, s, c, v, w)
                nc.vector.quantize_mx(
                    out=words[s][:, c0 : c0 + w].bitcast(FP8X4),
                    scales=scales[s][:, c0 : c0 + w],
                    in_=grouped[s, c][:].rearrange("p w j -> p (w j)"),
                )

        slot_words, slot_scales, hq, hqs, ys = {}, {}, {}, {}, {}

        def gather(n):
            for s in range(PASSES):
                for g, (lo, w) in enumerate(GROUPS[s]):
                    if lo == UNITS[n][0]:
                        index = offs_t[:, lo // 16 : (lo + w) // 16]
                        slot_words[s, g] = tile(f"W{s}_{g}", [P, w], U32)
                        slot_scales[s, g] = tile(f"B{s}_{g}", [P, w], U8)
                        nc.vector.tensor_copy(slot_words[s, g][:], words[s][:].indirect(index))
                        nc.vector.tensor_copy(slot_scales[s, g][:], scales[s][:].indirect(index))

        def of_slots(tiles, s, lo):
            for g, (g0, w) in enumerate(GROUPS[s]):
                if g0 <= lo < g0 + w:
                    return tiles[s, g][:, lo - g0 : lo - g0 + P]

        def first(n):
            lo, w = UNITS[n]
            hs = []
            for b in range(w // P):
                e = (lo + P * b) // C
                acc = psum_a.tile([P, H], F32, name="acc")
                for s in range(PASSES):
                    nc.tensor.matmul_mx(
                        out=acc[:],
                        lhsT=of_slots(slot_words, s, lo + P * b).bitcast(FP8X4),
                        lhsT_scale=of_slots(slot_scales, s, lo + P * b),
                        rhs=w1w[:, 2 * e + s, :].bitcast(FP4X4),
                        rhs_scale=w1s[:, 2 * e + s, :],
                        start=(s == 0),
                        stop=(s == PASSES - 1),
                    )
                hs.append(tile(f"hs{n}_{b}", [P, 2, P, 2], BF16))
                nc.scalar.activation(hs[b][:], acc[:].rearrange("c (p u e) -> c u p e", u=2, e=2), RELU)
            hg = tile(f"hg{n}", [P, w, 4], BF16)
            hg_words = hg[:].rearrange("p c t -> p (c t)").bitcast(F32).rearrange("p (c u) -> p c u", u=2)
            for half in range(w // 256):
                k = (lo + 256 * half) // 256
                tp = psum_b.tile([P, 2, 256], F32, name=f"tp{k}", tag=f"bank{k % 4}")
                for b in range(2):
                    turned = hs[2 * half + b][:].rearrange("c u p e -> c u (p e)").bitcast(F32)
                    for u in range(2):
                        nc.tensor.transpose(tp[:, u, P * b : P * b + P], turned[:, u, :], ident[:])
                nc.scalar.copy(hg_words[:, 256 * half : 256 * half + 256, :], tp[:].rearrange("p u r -> p r u"))
            hq[n] = tile(f"hq{n}", [P, w], U32)
            hqs[n] = tile(f"hqs{n}", [P, w], U8)
            nc.vector.quantize_mx(out=hq[n][:].bitcast(FP8X4), scales=hqs[n][:], in_=hg[:].rearrange("p c t -> p (c t)"))

        def second(n):
            lo, w = UNITS[n]
            y = psum_b.tile([P, 512], F32, name=f"y{n}", tag=f"bank{YBANK[n]}")
            for b in range(w // C):
                e = lo // C + b
                cols = slice(C * b, C * b + C)
                nc.tensor.matmul_mx(
                    out=y[:, cols],
                    lhsT=w2w[:, e, :].bitcast(FP4X4),
                    lhsT_scale=w2s[:, e, :],
                    rhs=hq[n][:, cols].bitcast(FP8X4),
                    rhs_scale=hqs[n][:, cols],
                    start=True,
                    stop=True,
                )
            for g, (g0, gw) in enumerate(SCATTERS):
                if g0 <= lo < g0 + gw:
                    if g not in ys:
                        ys[g] = tile(f"ys{g}", [P, gw], F32)
                    nc.scalar.copy(ys[g][:, lo - g0 : lo - g0 + w], y[:, :w])

        for n in range(len(UNITS)):
            gather(n)
            first(n)
            if n >= 1:
                second(n - 1)
        second(len(UNITS) - 1)
        for g, (lo, w) in enumerate(SCATTERS):
            nc.vector.tensor_tensor(out_t[:].indirect(dst_t[:, lo // 16 : (lo + w) // 16]), ys[g][:], gate_t[:, lo : lo + w], MULT)
        nc.sync.dma_start(out=out, in_=out_t[:])
